import numpy as np
import ml_dtypes


def mxq(x, axis, fmt="e4m3"):
    dtype, down = {"e4m3": (ml_dtypes.float8_e4m3fn, 7), "e5m2": (ml_dtypes.float8_e5m2, 14)}[fmt]
    v = np.moveaxis(np.asarray(x, np.float32).astype(ml_dtypes.bfloat16).astype(np.float64), axis, -1)
    blocks = v.reshape(v.shape[:-1] + (-1, 32))
    amax = np.abs(blocks).max(-1, keepdims=True)
    byte = np.maximum(np.where(amax > 0, np.frexp(amax)[1] - 1 + 127, 0) - down, 1)
    scale = np.exp2(byte - 127.0)
    codes = (blocks / scale).astype(np.float32).astype(dtype).astype(np.float64)
    return np.moveaxis((codes * scale).reshape(v.shape), -1, axis)


WIDE = False


def mx_kscale(k):
    if not WIDE:
        return np.ones(k)
    levels = np.array([30, -30])
    if k % 512:
        return np.exp2(np.random.permutation(np.resize(levels, k // 32))).repeat(32)
    a = np.empty((k // 512, 16))
    for p in range(k // 512):
        a[p, :8] = np.random.permutation(np.resize(levels, 8))
        for g in range(8):
            far = levels[np.abs(levels - a[p, g]) >= 10]
            a[p, g + 8] = far[np.random.randint(len(far))]
    return np.exp2(a.ravel()).repeat(32)


def f64(x):
    return np.asarray(x).astype(np.float64)


def striped8(idx):
    return np.asarray(idx).reshape(8, -1, 16).transpose(0, 2, 1).reshape(128, -1).astype(np.uint16)


def unstriped8(offs):
    return offs.reshape(8, 16, -1).transpose(0, 2, 1).reshape(8, -1).astype(np.int64)


def pick8(x, idx, run):
    r = np.arange(len(x))
    return x[r[:, None], idx[r % (8 * run) // run]]


E2M1 = np.array([0.0, 0.5, 1.0, 1.5, 2.0, 3.0, 4.0, 6.0, -0.0, -0.5, -1.0, -1.5, -2.0, -3.0, -4.0, -6.0])


def pack_weight(w, fmt):
    k, n = w.shape
    w = f64(np.asarray(w, np.float32).astype(ml_dtypes.bfloat16)).reshape(k // 32, 32, n)
    amax = np.abs(w).max(1)
    if fmt in ("e4m3", "e5m2"):
        byte = np.frexp(amax)[1] - 1 + 127 - (7 if fmt == "e4m3" else 14)
    else:
        mant, ex = np.frexp(amax / 6.0)
        byte = np.where(mant > 0.5, ex, ex - 1) + 127
    byte = np.clip(np.where(amax > 0, byte, 1), 1, 254)
    scaled = (w * np.exp2(127.0 - byte)[:, None, :]).reshape(k, n).astype(np.float32)
    by_word = np.ascontiguousarray(scaled.reshape(k // 512, 128, 4, n).transpose(0, 1, 3, 2))
    if fmt in ("e4m3", "e5m2"):
        words = by_word.astype(ml_dtypes.float8_e4m3fn if fmt == "e4m3" else ml_dtypes.float8_e5m2).view(np.uint8)
    else:
        c = by_word.astype(ml_dtypes.float4_e2m1fn).view(np.uint8) & 0xF
        words = (c[..., 0::2] | (c[..., 1::2] << 4)).reshape(k // 512, 128, 2 * n)
    return np.ascontiguousarray(words), np.ascontiguousarray(byte.astype(np.uint8).reshape(k // 512, 16, n))


def unpack_weight(words, scales, fmt):
    g, _, n = scales.shape
    words = np.ascontiguousarray(words).reshape(g, 128, n, -1)
    if fmt in ("e4m3", "e5m2"):
        vals = words.view(ml_dtypes.float8_e4m3fn if fmt == "e4m3" else ml_dtypes.float8_e5m2).astype(np.float64)
    else:
        nib = np.empty((g, 128, n, 4), np.uint8)
        nib[..., 0::2] = words & 0xF
        nib[..., 1::2] = words >> 4
        vals = E2M1[nib]
    vals = vals * np.repeat(np.exp2(scales.astype(np.float64) - 127.0), 8, axis=1)[..., None]
    return vals.transpose(0, 1, 3, 2).reshape(g * 512, n)


K, T, J, R, N = 1024, 512, 256, 512, 256


def setup_inputs():
    n = np.random.standard_normal
    idx = np.stack([np.random.permutation(T)[:J] for _ in range(8)])
    fk = mx_kscale(K)
    fr = mx_kscale(R)
    xtp = pack_weight(n((K, T)) / fk[:, None], "e4m3")
    wp = pack_weight(n((K, R)) * 1 / np.sqrt(K) * fk[:, None] * fr, "e2m1")
    wbp = pack_weight(n((R, N)) * 1 / np.sqrt(R) / fr[:, None], "e5m2")
    return {
        "xt_words": xtp[0],
        "xt_scales": xtp[1],
        "w_words": wp[0],
        "w_scales": wp[1],
        "us": (np.random.uniform(0.5, 2.0, (R, 1)) * fr[:, None]).astype(np.float32),
        "wb_words": wbp[0],
        "wb_scales": wbp[1],
        "rs": (n((N, J))).astype(np.float32),
        "gm": (np.random.uniform(0.5, 2.0, (N, 1))).astype(np.float32),
        "offs": striped8(idx),
    }


def reference(xt_words, xt_scales, w_words, w_scales, us, wb_words, wb_scales, rs, gm, offs):
    idx = unstriped8(offs)
    xtu = unpack_weight(xt_words, xt_scales, "e4m3")
    wu = unpack_weight(w_words, w_scales, "e2m1")
    wbu = unpack_weight(wb_words, wb_scales, "e5m2")
    xtidxg = pick8(xtu, idx, 64)
    a = wu.T @ xtidxg
    pk1 = np.max(np.abs(a), axis=1, keepdims=True)
    hid = a / pk1 * f64(us)
    hidq = mxq(hid, 0, "e5m2")
    p = wbu.T @ hidq
    y = f64(gm) * p + f64(rs)
    return y

@@ -1,0 +1,154 @@
+from contextlib import ExitStack
+
+import concourse.mybir as mybir
+
+K, T, J, R, N = 1024, 512, 256, 512, 256
+FLOPS = 2 * K * R * J + 2 * R * N * J
+
+F32 = mybir.dt.float32
+BF16 = mybir.dt.bfloat16
+I32 = mybir.dt.int32
+U32 = mybir.dt.uint32
+U16 = mybir.dt.uint16
+U8 = mybir.dt.uint8
+E4M3 = mybir.dt.float8_e4m3fn_x4
+E5M2 = mybir.dt.float8_e5m2_x4
+E2M1 = mybir.dt.float4_e2m1fn_x4
+ALU = mybir.AluOpType
+P = 128
+HALF = J // 2
+
+
+def tile_list_headpicks_peakscaled_residual_kernel(tc, xt_words, xt_scales, w_words, w_scales, us, wb_words, wb_scales, rs, gm, offs, out):
+    nc = tc.nc
+    with ExitStack() as ctx:
+        keep = ctx.enter_context(tc.tile_pool(name="keep", bufs=1))
+        psum = ctx.enter_context(tc.psum_pool(name="psum", bufs=1))
+        queues = (nc.sync, nc.scalar)
+
+        offsets = keep.tile([P, J // 16], U16, name="offsets")
+        nc.sync.dma_start(offsets[:], offs)
+
+        xs_window = keep.tile([P, T], U8, name="xs_window", tag="xs_then_wb", align_bytes=64)
+        nc.gpsimd.memset(xs_window[:].bitcast(I32), 0)
+        ws_raw = keep.tile([P, 2 * R], U8, name="ws_raw", align_bytes=64)
+        nc.vector.memset(ws_raw[:].bitcast(I32), 0)
+        x_planes = [keep.tile([P, J], U8, name="x_plane%d" % z, align_bytes=64) for z in range(2)]
+        for z in range(2):
+            nc.vector.memset(x_planes[z][:].bitcast(I32), 0)
+
+        nc.scalar.dma_start(xs_window[:].bitcast(I32)[0::4, :], xt_scales.rearrange("z q c -> q z c").bitcast(I32))
+        w_raw = keep.tile([P, 2, 2 * R], U8, name="w_raw", tag="w_then_rs", align_bytes=64)
+        nc.sync.dma_start(w_raw[:].bitcast(I32), w_words.rearrange("z p b -> p z b").bitcast(I32))
+        x_windows = [keep.tile([P, T], I32, name="x_window%d" % z, align_bytes=64) for z in range(2)]
+        nc.sync.dma_start(x_windows[0][:], xt_words[0].rearrange("p c b -> p (c b)").bitcast(I32))
+        nc.gpsimd.dma_start(x_windows[1][:], xt_words[1].rearrange("p c b -> p (c b)").bitcast(I32))
+        for quad in range(4):
+            nc.scalar.dma_start(
+                ws_raw[:].bitcast(I32)[32 * quad : 32 * quad + 4, :].rearrange("p (z c) -> p z c", z=2),
+                w_scales[:, 4 * quad : 4 * quad + 4, :].rearrange("z q c -> q z c").bitcast(I32),
+            )
+        us_sb = keep.tile([P, 4], F32, name="us_sb")
+        nc.gpsimd.dma_start(us_sb[:], us.rearrange("(p t) o -> p (t o)", t=4))
+
+        xs_picked = keep.tile([P, J], U8, name="xs_picked", tag="picked_then_gm", align_bytes=64)
+        nc.vector.tensor_copy(xs_picked[:], xs_window[:].indirect(offsets[:]))
+        for z in range(2):
+            for quad in range(4):
+                queues[quad % 2].dma_start(
+                    x_planes[z][:].bitcast(I32)[32 * quad : 32 * quad + 4, :],
+                    xs_picked[:].bitcast(I32)[32 * quad + 4 * z : 32 * quad + 32 : 8, :],
+                )
+
+        acc = [psum.tile([P, J], F32, name="acc%d" % t) for t in range(4)]
+        for z in range(2):
+            w_dealt = keep.tile([P, 2 * R], U8, name="w_dealt%d" % z, align_bytes=64)
+            nc.vector.tensor_copy(
+                w_dealt[:].bitcast(U16).rearrange("p (t c i) -> p c t i", t=4, i=8),
+                w_raw[:, z, :].bitcast(U16).rearrange("p (c i t) -> p c t i", t=4, i=8),
+            )
+            ws_dealt = keep.tile([P, R], U8, name="ws_dealt%d" % z, align_bytes=64)
+            nc.vector.tensor_copy(
+                ws_dealt[:].rearrange("p (t c i) -> p c t i", t=4, i=16),
+                ws_raw[:, z * R : (z + 1) * R].rearrange("p (c i t) -> p c t i", t=4, i=16),
+            )
+            x_picked = keep.tile([P, J], U32, name="x_picked%d" % z, align_bytes=64)
+            nc.vector.tensor_copy(x_picked[:], x_windows[z][:].bitcast(U32).indirect(offsets[:]))
+            for t in range(4):
+                nc.tensor.matmul_mx(
+                    acc[t][:],
+                    lhsT=w_dealt[:, 256 * t : 256 * (t + 1)].bitcast(E2M1),
+                    lhsT_scale=ws_dealt[:, P * t : P * (t + 1)],
+                    rhs=x_picked[:].bitcast(E4M3),
+                    rhs_scale=x_planes[z][:],
+                    start=(z == 0),
+                    stop=(z == 1),
+                )
+
+        wb_sb = keep.tile([P, N], I32, name="wb_sb", tag="xs_then_wb", align_bytes=64)
+        nc.sync.dma_start(wb_sb[:], wb_words[0].rearrange("p c b -> p (c b)").bitcast(I32))
+        for quad in range(4):
+            nc.sync.dma_start(
+                ws_raw[:].bitcast(I32)[32 * quad : 32 * quad + 4, 0 : N // 4],
+                wb_scales[0, 4 * quad : 4 * quad + 4, :].bitcast(I32),
+            )
+        rs_sb = keep.tile([P, 2, J], F32, name="rs_sb", tag="w_then_rs", align_bytes=64)
+        nc.sync.dma_start(rs_sb[:], rs.rearrange("(u p) j -> p u j", p=P))
+        gm_sb = keep.tile([P, 2], F32, name="gm_sb", tag="picked_then_gm", align_bytes=64)
+        with nc.allow_non_contiguous_dma(reason="one factor for each output row"):
+            nc.sync.dma_start(gm_sb[:], gm.rearrange("(u p) o -> p (u o)", p=P))
+
+        a_sb = [keep.tile([P, J], F32, name="a_sb%d" % t) for t in range(4)]
+        peak = keep.tile([P, 4], F32, name="peak")
+        inv = keep.tile([P, 4], F32, name="inv")
+        hid_planes = keep.tile([P, 4, J], BF16, name="hid_planes", align_bytes=64)
+
+        def find_peak(t):
+            nc.scalar.copy(a_sb[t][:], acc[t][:])
+            nc.vector.tensor_reduce(peak[:, t : t + 1], a_sb[t][:], mybir.AxisListType.X, ALU.max, apply_absolute_value=True)
+
+        def scale(t):
+            nc.vector.tensor_scalar(hid_planes[:, t, :], a_sb[t][:], inv[:, t : t + 1], us_sb[:, t : t + 1], ALU.mult, ALU.mult)
+
+        find_peak(0)
+        find_peak(1)
+        find_peak(2)
+        nc.vector.reciprocal(inv[:, 0:2], peak[:, 0:2])
+        find_peak(3)
+        scale(0)
+        nc.vector.reciprocal(inv[:, 2:4], peak[:, 2:4])
+        scale(1)
+        scale(2)
+        scale(3)
+
+        woven = []
+        for h in range(2):
+            hid = keep.tile([P, 4 * HALF], BF16, name="hid%d" % h, align_bytes=64)
+            nc.vector.tensor_copy(
+                hid[:].rearrange("p (c i t) -> p c t i", t=4, i=4),
+                hid_planes[:, :, h * HALF : (h + 1) * HALF].rearrange("p t (c i) -> p c t i", i=4),
+            )
+            woven.append(hid)
+        prods = []
+        for h in range(2):
+            codes = keep.tile([P, HALF], U32, name="codes%d" % h, align_bytes=64)
+            plane = keep.tile([P, HALF], U8, name="plane%d" % h, align_bytes=64)
+            nc.vector.quantize_mx(codes[:].bitcast(E5M2), plane[:], woven[h][:])
+            for u in range(2):
+                prod = psum.tile([P, HALF], F32, name="prod%d%d" % (h, u))
+                nc.tensor.matmul_mx(
+                    prod[:],
+                    lhsT=wb_sb[:, P * u : P * (u + 1)].bitcast(E5M2),
+                    lhsT_scale=ws_raw[:, P * u : P * (u + 1)],
+                    rhs=codes[:].bitcast(E5M2),
+                    rhs_scale=plane[:],
+                    start=True,
+                    stop=True,
+                )
+                prods.append(prod)
+        for h in range(2):
+            cols = slice(h * HALF, (h + 1) * HALF)
+            res = keep.tile([P, 2, HALF], F32, name="res%d" % h)
+            for u in range(2):
+                nc.vector.scalar_tensor_tensor(res[:, u, :], prods[2 * h + u][:], gm_sb[:, u : u + 1], rs_sb[:, u, cols], ALU.mult, ALU.add)
+            queues[h].dma_start(out.rearrange("(u p) j -> p u j", p=P)[:, :, cols], res[:])

@@ -23,41 +23,42 @@ def tile_list_headpicks_peakscaled_residual_kernel(tc, xt_words, xt_scales, w_wo
     nc = tc.nc
     with ExitStack() as ctx:
         keep = ctx.enter_context(tc.tile_pool(name="keep", bufs=1))
+        reused = ctx.enter_context(tc.tile_pool(name="reused", bufs=1))
         psum = ctx.enter_context(tc.psum_pool(name="psum", bufs=1))
         queues = (nc.sync, nc.scalar)
 
         offsets = keep.tile([P, J // 16], U16, name="offsets")
         nc.sync.dma_start(offsets[:], offs)
 
-        xs_window = keep.tile([P, T], U8, name="xs_window", tag="xs_then_wb", align_bytes=64)
-        nc.gpsimd.memset(xs_window[:].bitcast(I32), 0)
         ws_raw = keep.tile([P, 2 * R], U8, name="ws_raw", align_bytes=64)
         nc.vector.memset(ws_raw[:].bitcast(I32), 0)
         x_planes = [keep.tile([P, J], U8, name="x_plane%d" % z, align_bytes=64) for z in range(2)]
         for z in range(2):
             nc.vector.memset(x_planes[z][:].bitcast(I32), 0)
 
-        nc.scalar.dma_start(xs_window[:].bitcast(I32)[0::4, :], xt_scales.rearrange("z q c -> q z c").bitcast(I32))
-        w_raw = keep.tile([P, 2, 2 * R], U8, name="w_raw", tag="w_then_rs", align_bytes=64)
+        xs_window = keep.tile([P, T], U8, name="xs_window", align_bytes=64)
+        for z in range(2):
+            queues[z].dma_start(xs_window[:].bitcast(I32)[z::2, :], xt_scales[z].bitcast(I32).unsqueeze(1).to_broadcast([16, 4, T // 4]))
+        w_raw = keep.tile([P, 2, 2 * R], U8, name="w_raw", align_bytes=64)
         nc.sync.dma_start(w_raw[:].bitcast(I32), w_words.rearrange("z p b -> p z b").bitcast(I32))
-        x_windows = [keep.tile([P, T], I32, name="x_window%d" % z, align_bytes=64) for z in range(2)]
-        nc.sync.dma_start(x_windows[0][:], xt_words[0].rearrange("p c b -> p (c b)").bitcast(I32))
-        nc.gpsimd.dma_start(x_windows[1][:], xt_words[1].rearrange("p c b -> p (c b)").bitcast(I32))
         for quad in range(4):
             nc.scalar.dma_start(
                 ws_raw[:].bitcast(I32)[32 * quad : 32 * quad + 4, :].rearrange("p (z c) -> p z c", z=2),
                 w_scales[:, 4 * quad : 4 * quad + 4, :].rearrange("z q c -> q z c").bitcast(I32),
             )
+        x_windows = [keep.tile([P, T], I32, name="x_window%d" % z, align_bytes=64) for z in range(2)]
+        for z in range(2):
+            nc.sync.dma_start(x_windows[z][:], xt_words[z].rearrange("p c b -> p (c b)").bitcast(I32))
         us_sb = keep.tile([P, 4], F32, name="us_sb")
         nc.gpsimd.dma_start(us_sb[:], us.rearrange("(p t) o -> p (t o)", t=4))
 
-        xs_picked = keep.tile([P, J], U8, name="xs_picked", tag="picked_then_gm", align_bytes=64)
+        xs_picked = reused.tile([P, J], U8, name="xs_picked", offset=960, align_bytes=64)
         nc.vector.tensor_copy(xs_picked[:], xs_window[:].indirect(offsets[:]))
         for z in range(2):
             for quad in range(4):
                 queues[quad % 2].dma_start(
                     x_planes[z][:].bitcast(I32)[32 * quad : 32 * quad + 4, :],
-                    xs_picked[:].bitcast(I32)[32 * quad + 4 * z : 32 * quad + 32 : 8, :],
+                    xs_picked[:].bitcast(I32)[32 * quad + z : 32 * quad + 32 : 8, :],
                 )
 
         acc = [psum.tile([P, J], F32, name="acc%d" % t) for t in range(4)]
@@ -67,13 +68,13 @@ def tile_list_headpicks_peakscaled_residual_kernel(tc, xt_words, xt_scales, w_wo
                 w_dealt[:].bitcast(U16).rearrange("p (t c i) -> p c t i", t=4, i=8),
                 w_raw[:, z, :].bitcast(U16).rearrange("p (c i t) -> p c t i", t=4, i=8),
             )
+            x_picked = keep.tile([P, J], U32, name="x_picked%d" % z, align_bytes=64)
+            nc.vector.tensor_copy(x_picked[:], x_windows[z][:].bitcast(U32).indirect(offsets[:]))
             ws_dealt = keep.tile([P, R], U8, name="ws_dealt%d" % z, align_bytes=64)
             nc.vector.tensor_copy(
                 ws_dealt[:].rearrange("p (t c i) -> p c t i", t=4, i=16),
                 ws_raw[:, z * R : (z + 1) * R].rearrange("p (c i t) -> p c t i", t=4, i=16),
             )
-            x_picked = keep.tile([P, J], U32, name="x_picked%d" % z, align_bytes=64)
-            nc.vector.tensor_copy(x_picked[:], x_windows[z][:].bitcast(U32).indirect(offsets[:]))
             for t in range(4):
                 nc.tensor.matmul_mx(
                     acc[t][:],
@@ -85,16 +86,16 @@ def tile_list_headpicks_peakscaled_residual_kernel(tc, xt_words, xt_scales, w_wo
                     stop=(z == 1),
                 )
 
-        wb_sb = keep.tile([P, N], I32, name="wb_sb", tag="xs_then_wb", align_bytes=64)
+        wb_sb = reused.tile([P, N], I32, name="wb_sb", offset=0, align_bytes=64)
         nc.sync.dma_start(wb_sb[:], wb_words[0].rearrange("p c b -> p (c b)").bitcast(I32))
         for quad in range(4):
             nc.sync.dma_start(
-                ws_raw[:].bitcast(I32)[32 * quad : 32 * quad + 4, 0 : N // 4],
+                ws_raw[:].bitcast(I32)[32 * quad : 32 * quad + 4, R // 4 : R // 4 + N // 4],
                 wb_scales[0, 4 * quad : 4 * quad + 4, :].bitcast(I32),
             )
-        rs_sb = keep.tile([P, 2, J], F32, name="rs_sb", tag="w_then_rs", align_bytes=64)
+        rs_sb = reused.tile([P, 2, J], F32, name="rs_sb", offset=1152, align_bytes=64)
         nc.sync.dma_start(rs_sb[:], rs.rearrange("(u p) j -> p u j", p=P))
-        gm_sb = keep.tile([P, 2], F32, name="gm_sb", tag="picked_then_gm", align_bytes=64)
+        gm_sb = reused.tile([P, 2], F32, name="gm_sb", offset=1024, align_bytes=64)
         with nc.allow_non_contiguous_dma(reason="one factor for each output row"):
             nc.sync.dma_start(gm_sb[:], gm.rearrange("(u p) o -> p (u o)", p=P))
 
@@ -107,28 +108,38 @@ def tile_list_headpicks_peakscaled_residual_kernel(tc, xt_words, xt_scales, w_wo
             nc.scalar.copy(a_sb[t][:], acc[t][:])
             nc.vector.tensor_reduce(peak[:, t : t + 1], a_sb[t][:], mybir.AxisListType.X, ALU.max, apply_absolute_value=True)
 
-        def scale(t):
-            nc.vector.tensor_scalar(hid_planes[:, t, :], a_sb[t][:], inv[:, t : t + 1], us_sb[:, t : t + 1], ALU.mult, ALU.mult)
+        def scale(t, lo=0, hi=J):
+            nc.vector.tensor_scalar(hid_planes[:, t, lo:hi], a_sb[t][:, lo:hi], inv[:, t : t + 1], us_sb[:, t : t + 1], ALU.mult, ALU.mult)
+
+        def invert(lo, hi):
+            nc.vector.reciprocal(inv[:, lo:hi], peak[:, lo:hi])
 
         find_peak(0)
         find_peak(1)
         find_peak(2)
-        nc.vector.reciprocal(inv[:, 0:2], peak[:, 0:2])
+        invert(0, 2)
         find_peak(3)
+        invert(2, 3)
         scale(0)
-        nc.vector.reciprocal(inv[:, 2:4], peak[:, 2:4])
+        invert(3, 4)
         scale(1)
         scale(2)
-        scale(3)
+        scale(3, 0, HALF)
+        scale(3, HALF, J)
 
-        woven = []
-        for h in range(2):
-            hid = keep.tile([P, 4 * HALF], BF16, name="hid%d" % h, align_bytes=64)
-            nc.vector.tensor_copy(
-                hid[:].rearrange("p (c i t) -> p c t i", t=4, i=4),
-                hid_planes[:, :, h * HALF : (h + 1) * HALF].rearrange("p t (c i) -> p c t i", i=4),
+        woven = [keep.tile([P, 4 * HALF], BF16, name="hid%d" % h, align_bytes=64) for h in range(2)]
+
+        def weave(copy, lo, hi):
+            h, at = divmod(lo, HALF)
+            copy(
+                woven[h][:, 4 * at : 4 * (at + hi - lo)].rearrange("p (c i t) -> p c t i", t=4, i=4),
+                hid_planes[:, :, lo:hi].rearrange("p t (c i) -> p c t i", i=4),
             )
-            woven.append(hid)
+
+        weave(nc.vector.tensor_copy, 0, 96)
+        weave(nc.scalar.copy, 96, 128)
+        weave(nc.vector.tensor_copy, 128, 208)
+        weave(nc.scalar.copy, 208, 256)
         prods = []
         for h in range(2):
             codes = keep.tile([P, HALF], U32, name="codes%d" % h, align_bytes=64)
@@ -139,7 +150,7 @@ def tile_list_headpicks_peakscaled_residual_kernel(tc, xt_words, xt_scales, w_wo
                 nc.tensor.matmul_mx(
                     prod[:],
                     lhsT=wb_sb[:, P * u : P * (u + 1)].bitcast(E5M2),
-                    lhsT_scale=ws_raw[:, P * u : P * (u + 1)],
+                    lhsT_scale=ws_raw[:, R + P * u : R + P * (u + 1)],
                     rhs=codes[:].bitcast(E5M2),
                     rhs_scale=plane[:],
                     start=True,
@@ -151,4 +162,4 @@ def tile_list_headpicks_peakscaled_residual_kernel(tc, xt_words, xt_scales, w_wo
             res = keep.tile([P, 2, HALF], F32, name="res%d" % h)
             for u in range(2):
                 nc.vector.scalar_tensor_tensor(res[:, u, :], prods[2 * h + u][:], gm_sb[:, u : u + 1], rs_sb[:, u, cols], ALU.mult, ALU.add)
-            queues[h].dma_start(out.rearrange("(u p) j -> p u j", p=P)[:, :, cols], res[:])
+                queues[u].dma_start(out[P * u : P * (u + 1), cols], res[:, u, :])

@@ -33,12 +33,11 @@ def tile_list_headpicks_peakscaled_residual_kernel(tc, xt_words, xt_scales, w_wo
         ws_raw = keep.tile([P, 2 * R], U8, name="ws_raw", align_bytes=64)
         nc.vector.memset(ws_raw[:].bitcast(I32), 0)
         x_planes = [keep.tile([P, J], U8, name="x_plane%d" % z, align_bytes=64) for z in range(2)]
-        for z in range(2):
-            nc.vector.memset(x_planes[z][:].bitcast(I32), 0)
+        nc.vector.memset(x_planes[0][:].bitcast(I32), 0)
 
         xs_window = keep.tile([P, T], U8, name="xs_window", align_bytes=64)
         for z in range(2):
-            queues[z].dma_start(xs_window[:].bitcast(I32)[z::2, :], xt_scales[z].bitcast(I32).unsqueeze(1).to_broadcast([16, 4, T // 4]))
+            queues[z].dma_start(xs_window[:].bitcast(I32)[1 - z :: 2, :], xt_scales[z].bitcast(I32).unsqueeze(1).to_broadcast([16, 4, T // 4]))
         w_raw = keep.tile([P, 2, 2 * R], U8, name="w_raw", align_bytes=64)
         nc.sync.dma_start(w_raw[:].bitcast(I32), w_words.rearrange("z p b -> p z b").bitcast(I32))
         for quad in range(4):
@@ -54,12 +53,14 @@ def tile_list_headpicks_peakscaled_residual_kernel(tc, xt_words, xt_scales, w_wo
 
         xs_picked = reused.tile([P, J], U8, name="xs_picked", offset=960, align_bytes=64)
         nc.vector.tensor_copy(xs_picked[:], xs_window[:].indirect(offsets[:]))
-        for z in range(2):
-            for quad in range(4):
-                queues[quad % 2].dma_start(
-                    x_planes[z][:].bitcast(I32)[32 * quad : 32 * quad + 4, :],
-                    xs_picked[:].bitcast(I32)[32 * quad + z : 32 * quad + 32 : 8, :],
-                )
+        for quad in range(4):
+            queues[quad % 2].dma_start(
+                x_planes[0][:].bitcast(I32)[32 * quad : 32 * quad + 4, :],
+                xs_picked[:].bitcast(I32)[32 * quad + 1 : 32 * quad + 32 : 8, :],
+            )
+        nc.vector.tensor_copy(x_planes[1][:].bitcast(I32), xs_picked[:].bitcast(I32))
+        for row in range(1, 4):
+            queues[row % 2].dma_start(x_planes[1][:].bitcast(I32)[row::32, :], xs_picked[:].bitcast(I32)[8 * row :: 32, :])
 
         acc = [psum.tile([P, J], F32, name="acc%d" % t) for t in range(4)]
         for z in range(2):

from contextlib import ExitStack

import concourse.mybir as mybir

K, T, J, R, N = 1024, 512, 256, 512, 256
FLOPS = 2 * K * R * J + 2 * R * N * J

F32 = mybir.dt.float32
BF16 = mybir.dt.bfloat16
I32 = mybir.dt.int32
U32 = mybir.dt.uint32
U16 = mybir.dt.uint16
U8 = mybir.dt.uint8
E4M3 = mybir.dt.float8_e4m3fn_x4
E5M2 = mybir.dt.float8_e5m2_x4
E2M1 = mybir.dt.float4_e2m1fn_x4
ALU = mybir.AluOpType
P = 128
HALF = J // 2


def tile_list_headpicks_peakscaled_residual_kernel(tc, xt_words, xt_scales, w_words, w_scales, us, wb_words, wb_scales, rs, gm, offs, out):
    nc = tc.nc
    with ExitStack() as ctx:
        keep = ctx.enter_context(tc.tile_pool(name="keep", bufs=1))
        reused = ctx.enter_context(tc.tile_pool(name="reused", bufs=1))
        psum = ctx.enter_context(tc.psum_pool(name="psum", bufs=1))
        queues = (nc.sync, nc.scalar)

        offsets = keep.tile([P, J // 16], U16, name="offsets")
        nc.sync.dma_start(offsets[:], offs)

        ws_raw = keep.tile([P, 2 * R], U8, name="ws_raw", align_bytes=64)
        nc.vector.memset(ws_raw[:].bitcast(I32), 0)
        x_planes = [keep.tile([P, J], U8, name="x_plane%d" % z, align_bytes=64) for z in range(2)]
        nc.vector.memset(x_planes[0][:].bitcast(I32), 0)

        xs_window = keep.tile([P, T], U8, name="xs_window", align_bytes=64)
        for z in range(2):
            queues[z].dma_start(xs_window[:].bitcast(I32)[1 - z :: 2, :], xt_scales[z].bitcast(I32).unsqueeze(1).to_broadcast([16, 4, T // 4]))
        w_raw = keep.tile([P, 2, 2 * R], U8, name="w_raw", align_bytes=64)
        nc.sync.dma_start(w_raw[:].bitcast(I32), w_words.rearrange("z p b -> p z b").bitcast(I32))
        for quad in range(4):
            nc.scalar.dma_start(
                ws_raw[:].bitcast(I32)[32 * quad : 32 * quad + 4, :].rearrange("p (z c) -> p z c", z=2),
                w_scales[:, 4 * quad : 4 * quad + 4, :].rearrange("z q c -> q z c").bitcast(I32),
            )
        x_windows = [keep.tile([P, T], I32, name="x_window%d" % z, align_bytes=64) for z in range(2)]
        for z in range(2):
            nc.sync.dma_start(x_windows[z][:], xt_words[z].rearrange("p c b -> p (c b)").bitcast(I32))
        us_sb = keep.tile([P, 4], F32, name="us_sb")
        nc.gpsimd.dma_start(us_sb[:], us.rearrange("(p t) o -> p (t o)", t=4))

        xs_picked = reused.tile([P, J], U8, name="xs_picked", offset=960, align_bytes=64)
        nc.vector.tensor_copy(xs_picked[:], xs_window[:].indirect(offsets[:]))
        for quad in range(4):
            queues[quad % 2].dma_start(
                x_planes[0][:].bitcast(I32)[32 * quad : 32 * quad + 4, :],
                xs_picked[:].bitcast(I32)[32 * quad + 1 : 32 * quad + 32 : 8, :],
            )
        nc.vector.tensor_copy(x_planes[1][:].bitcast(I32), xs_picked[:].bitcast(I32))
        for row in range(1, 4):
            queues[row % 2].dma_start(x_planes[1][:].bitcast(I32)[row::32, :], xs_picked[:].bitcast(I32)[8 * row :: 32, :])

        acc = [psum.tile([P, J], F32, name="acc%d" % t) for t in range(4)]
        for z in range(2):
            w_dealt = keep.tile([P, 2 * R], U8, name="w_dealt%d" % z, align_bytes=64)
            nc.vector.tensor_copy(
                w_dealt[:].bitcast(U16).rearrange("p (t c i) -> p c t i", t=4, i=8),
                w_raw[:, z, :].bitcast(U16).rearrange("p (c i t) -> p c t i", t=4, i=8),
            )
            x_picked = keep.tile([P, J], U32, name="x_picked%d" % z, align_bytes=64)
            nc.vector.tensor_copy(x_picked[:], x_windows[z][:].bitcast(U32).indirect(offsets[:]))
            ws_dealt = keep.tile([P, R], U8, name="ws_dealt%d" % z, align_bytes=64)
            nc.vector.tensor_copy(
                ws_dealt[:].rearrange("p (t c i) -> p c t i", t=4, i=16),
                ws_raw[:, z * R : (z + 1) * R].rearrange("p (c i t) -> p c t i", t=4, i=16),
            )
            for t in range(4):
                nc.tensor.matmul_mx(
                    acc[t][:],
                    lhsT=w_dealt[:, 256 * t : 256 * (t + 1)].bitcast(E2M1),
                    lhsT_scale=ws_dealt[:, P * t : P * (t + 1)],
                    rhs=x_picked[:].bitcast(E4M3),
                    rhs_scale=x_planes[z][:],
                    start=(z == 0),
                    stop=(z == 1),
                )

        wb_sb = reused.tile([P, N], I32, name="wb_sb", offset=0, align_bytes=64)
        nc.sync.dma_start(wb_sb[:], wb_words[0].rearrange("p c b -> p (c b)").bitcast(I32))
        for quad in range(4):
            nc.sync.dma_start(
                ws_raw[:].bitcast(I32)[32 * quad : 32 * quad + 4, R // 4 : R // 4 + N // 4],
                wb_scales[0, 4 * quad : 4 * quad + 4, :].bitcast(I32),
            )
        rs_sb = reused.tile([P, 2, J], F32, name="rs_sb", offset=1152, align_bytes=64)
        nc.sync.dma_start(rs_sb[:], rs.rearrange("(u p) j -> p u j", p=P))
        gm_sb = reused.tile([P, 2], F32, name="gm_sb", offset=1024, align_bytes=64)
        with nc.allow_non_contiguous_dma(reason="one factor for each output row"):
            nc.sync.dma_start(gm_sb[:], gm.rearrange("(u p) o -> p (u o)", p=P))

        a_sb = [keep.tile([P, J], F32, name="a_sb%d" % t) for t in range(4)]
        peak = keep.tile([P, 4], F32, name="peak")
        inv = keep.tile([P, 4], F32, name="inv")
        hid_planes = keep.tile([P, 4, J], BF16, name="hid_planes", align_bytes=64)

        def find_peak(t):
            nc.scalar.copy(a_sb[t][:], acc[t][:])
            nc.vector.tensor_reduce(peak[:, t : t + 1], a_sb[t][:], mybir.AxisListType.X, ALU.max, apply_absolute_value=True)

        def scale(t, lo=0, hi=J):
            nc.vector.tensor_scalar(hid_planes[:, t, lo:hi], a_sb[t][:, lo:hi], inv[:, t : t + 1], us_sb[:, t : t + 1], ALU.mult, ALU.mult)

        def invert(lo, hi):
            nc.vector.reciprocal(inv[:, lo:hi], peak[:, lo:hi])

        find_peak(0)
        find_peak(1)
        find_peak(2)
        invert(0, 2)
        find_peak(3)
        invert(2, 3)
        scale(0)
        invert(3, 4)
        scale(1)
        scale(2)
        scale(3, 0, HALF)
        scale(3, HALF, J)

        woven = [keep.tile([P, 4 * HALF], BF16, name="hid%d" % h, align_bytes=64) for h in range(2)]

        def weave(copy, lo, hi):
            h, at = divmod(lo, HALF)
            copy(
                woven[h][:, 4 * at : 4 * (at + hi - lo)].rearrange("p (c i t) -> p c t i", t=4, i=4),
                hid_planes[:, :, lo:hi].rearrange("p t (c i) -> p c t i", i=4),
            )

        weave(nc.vector.tensor_copy, 0, 96)
        weave(nc.scalar.copy, 96, 128)
        weave(nc.vector.tensor_copy, 128, 208)
        weave(nc.scalar.copy, 208, 256)
        prods = []
        for h in range(2):
            codes = keep.tile([P, HALF], U32, name="codes%d" % h, align_bytes=64)
            plane = keep.tile([P, HALF], U8, name="plane%d" % h, align_bytes=64)
            nc.vector.quantize_mx(codes[:].bitcast(E5M2), plane[:], woven[h][:])
            for u in range(2):
                prod = psum.tile([P, HALF], F32, name="prod%d%d" % (h, u))
                nc.tensor.matmul_mx(
                    prod[:],
                    lhsT=wb_sb[:, P * u : P * (u + 1)].bitcast(E5M2),
                    lhsT_scale=ws_raw[:, R + P * u : R + P * (u + 1)],
                    rhs=codes[:].bitcast(E5M2),
                    rhs_scale=plane[:],
                    start=True,
                    stop=True,
                )
                prods.append(prod)
        for h in range(2):
            cols = slice(h * HALF, (h + 1) * HALF)
            res = keep.tile([P, 2, HALF], F32, name="res%d" % h)
            for u in range(2):
                nc.vector.scalar_tensor_tensor(res[:, u, :], prods[2 * h + u][:], gm_sb[:, u : u + 1], rs_sb[:, u, cols], ALU.mult, ALU.add)
                queues[u].dma_start(out[P * u : P * (u + 1), cols], res[:, u, :])
